import numpy as np
import ml_dtypes


def mxq(x, axis, fmt="e4m3"):
    dtype, down = {"e4m3": (ml_dtypes.float8_e4m3fn, 7), "e5m2": (ml_dtypes.float8_e5m2, 14)}[fmt]
    v = np.moveaxis(np.asarray(x, np.float32).astype(ml_dtypes.bfloat16).astype(np.float64), axis, -1)
    blocks = v.reshape(v.shape[:-1] + (-1, 32))
    amax = np.abs(blocks).max(-1, keepdims=True)
    byte = np.maximum(np.where(amax > 0, np.frexp(amax)[1] - 1 + 127, 0) - down, 1)
    scale = np.exp2(byte - 127.0)
    codes = (blocks / scale).astype(np.float32).astype(dtype).astype(np.float64)
    return np.moveaxis((codes * scale).reshape(v.shape), -1, axis)


WIDE = False


def mx_kscale(k):
    if not WIDE:
        return np.ones(k)
    levels = np.array([10, -10, 5, -5, 0])
    if k % 512:
        return np.exp2(np.random.permutation(np.resize(levels, k // 32))).repeat(32)
    a = np.empty((k // 512, 16))
    for p in range(k // 512):
        a[p, :8] = np.random.permutation(np.resize(levels, 8))
        for g in range(8):
            far = levels[np.abs(levels - a[p, g]) >= 10]
            a[p, g + 8] = far[np.random.randint(len(far))]
    return np.exp2(a.ravel()).repeat(32)


def f64(x):
    return np.asarray(x).astype(np.float64)


def striped(idx):
    return np.tile(np.asarray(idx).reshape(-1, 16).T, (8, 1)).astype(np.uint16)


def unstriped(offs):
    return offs[:16].T.reshape(-1).astype(np.int64)


B, N, T, D, DV, NQ = 2, 512, 2048, 512, 512, 128


def setup_inputs():
    n = np.random.standard_normal
    seg = T // B
    idx = np.concatenate([b * seg + np.random.permutation(seg)[:N] for b in range(B)])
    s = mx_kscale(D)[:, None]
    u = np.ones(T)
    u[idx] = mx_kscale(B * N)
    r = np.random.uniform(0.5, 2.0, T)
    raw = n((D, T)) / s / (u * r)
    return {
        "qT": (n((B, D, NQ)) * s * (0.60 / np.sqrt(D))).astype(np.float32),
        "cT": raw.astype(np.float32),
        "ts": np.tile(u * r, (128, 1)).astype(np.float32),
        "ch": np.tile(s[:, 0] * np.random.uniform(0.5, 2.0, D), (128, 1)).astype(np.float32),
        "og": n((B, NQ, DV)).astype(np.float32),
        "offs": striped(idx),
    }


def reference(qT, cT, ts, ch, og, offs):
    idx = unstriped(offs)
    c = f64(cT)
    pick = lambda x: x[:, idx].reshape(x.shape[0], B, N).transpose(1, 0, 2)
    q = f64(qT)
    score = mxq(q, 1, "e4m3").transpose(0, 2, 1) @ mxq(pick(c), 1, "e4m3")
    score = score * pick(f64(ts))[:, :1, :]
    m = score.max(-1, keepdims=True)
    p = np.exp(score - m)
    total = p.sum(-1, keepdims=True)
    w = p * pick(f64(ts))[:, :1, :]
    y = mxq(w, 2, "e4m3") @ mxq(pick(c).transpose(0, 2, 1), 1, "e4m3")
    y = y / total
    y = y * f64(ch)[:1]
    y = y / (1.0 + np.exp(-f64(og)))
    return y

@@ -1,0 +1,234 @@
+from contextlib import ExitStack
+
+import concourse.mybir as mybir
+from concourse.masks import make_identity
+
+FLOPS = 2 * 2 * 2 * 128 * 512 * 512
+
+F32 = mybir.dt.float32
+BF16 = mybir.dt.bfloat16
+U32 = mybir.dt.uint32
+U16 = mybir.dt.uint16
+U8 = mybir.dt.uint8
+FP8X4 = mybir.dt.float8_e4m3fn_x4
+MULT = mybir.AluOpType.mult
+ADD = mybir.AluOpType.add
+MAX = mybir.AluOpType.max
+COPY = mybir.ActivationFunctionType.Copy
+EXP = mybir.ActivationFunctionType.Exp
+TANH = mybir.ActivationFunctionType.Tanh
+AXIS_X = mybir.AxisListType.X
+
+P = 128
+B = 2
+N = 512
+T = 2048
+SEG = T // B
+D = 512
+NQ = 128
+HALF = SEG // 2
+ON_VECTOR = {(0, 0, 1), (1, 1, 1)}
+
+
+def tile_attend_x_mla_gate_seg_kernel(tc, qT, cT, ts, ch, og, offs, out):
+    nc = tc.nc
+    with ExitStack() as ctx:
+        lists = ctx.enter_context(tc.tile_pool(name="lists", bufs=1))
+        keep = ctx.enter_context(tc.tile_pool(name="keep", bufs=1))
+        psum = ctx.enter_context(tc.psum_pool(name="psum", bufs=1))
+
+        offsets = lists.tile([P, B * N // 16], U16, name="offsets")
+        nc.sync.dma_start(offsets[:], offs)
+
+        c_rows = cT.rearrange("(p t) n -> p t n", t=4)
+        raw = {}
+
+        def load_c(b, w, h):
+            piece = keep.tile([P, 2, HALF], F32, name=f"raw{b}{w}{h}")
+            n0 = b * SEG + h * HALF
+            nc.sync.dma_start(out=piece[:], in_=c_rows[:, 2 * w : 2 * w + 2, n0 : n0 + HALF])
+            raw[b, w, h] = piece
+
+        scale_tab = keep.tile([P, T], F32, name="scale_tab")
+        q_raw = keep.tile([P, B, 4, NQ], F32, name="q_raw")
+        ch_sb = keep.tile([P, D], F32, name="ch_sb")
+        og_sb = keep.tile([P, B, D], F32, name="og_sb")
+
+        def load_q(b):
+            nc.sync.dma_start(out=q_raw[:, b], in_=qT[b].rearrange("(p t) q -> p t q", t=4))
+
+        def load_ts(b):
+            nc.sync.dma_start(out=scale_tab[:, b * SEG : (b + 1) * SEG], in_=ts[:, b * SEG : (b + 1) * SEG])
+
+        load_ts(0)
+        for w in range(2):
+            for h in range(2):
+                load_c(0, w, h)
+        load_q(0)
+        load_c(1, 0, 0)
+        load_c(1, 0, 1)
+        load_ts(1)
+        load_c(1, 1, 0)
+        load_c(1, 1, 1)
+        load_q(1)
+        nc.sync.dma_start(out=ch_sb[:], in_=ch)
+        for b in range(B):
+            nc.sync.dma_start(out=og_sb[:, b, :], in_=og[b])
+
+        warm = keep.tile([P, 1], F32, name="warm")
+        nc.vector.memset(warm[:], 0.0)
+        warmed = keep.tile([P, 1], F32, name="warmed")
+        nc.scalar.activation(out=warmed[:], in_=warm[:], func=EXP)
+        ident = keep.tile([P, P], F32, name="ident")
+        make_identity(nc, ident[:])
+
+        pairs = [keep.tile([P, T, 2], BF16, name=f"pairs{w}", align_bytes=64) for w in range(2)]
+        q_bf = keep.tile([P, B, NQ, 4], BF16, name="q_bf", align_bytes=64)
+        q_codes = keep.tile([P, B * NQ], U32, name="q_codes", align_bytes=64)
+        q_scales = keep.tile([P, B * NQ], U8, name="q_scales", align_bytes=64)
+
+        def words(tile):
+            return tile[:].rearrange("p n e -> p (n e)").bitcast(U32)
+
+        kbf, tsg, p_sb, l_sum, ts_col = {}, {}, {}, {}, {}
+
+        def gather_latents(b):
+            kb = keep.tile([P, N, 4], BF16, name=f"kb{b}", align_bytes=64)
+            kbf[b] = kb
+            kw = kb[:].rearrange("p n t -> p (n t)").bitcast(U32).rearrange("p (n w) -> p w n", w=2)
+            for w in range(2):
+                for h in range(2):
+                    n0 = b * SEG + h * HALF
+                    dst = pairs[w][:, n0 : n0 + HALF, :]
+                    rd = raw[b, w, h][:].rearrange("p e n -> p n e")
+                    if (b, w, h) in ON_VECTOR:
+                        nc.vector.tensor_copy(out=dst, in_=rd)
+                    else:
+                        nc.scalar.activation(out=dst, in_=rd, func=COPY)
+                window = words(pairs[w])
+                if b == 0:
+                    window = window[:, 0:SEG]
+                nc.vector.tensor_copy(kw[:, w, :], window.indirect(offsets[:, b * (N // 16) : (b + 1) * (N // 16)]))
+
+        def gather_scales(b):
+            g = keep.tile([P, N], F32, name=f"tsg{b}")
+            window = scale_tab[:] if b else scale_tab[:, 0:SEG]
+            nc.vector.tensor_copy(g[:], window.indirect(offsets[:, b * (N // 16) : (b + 1) * (N // 16)]))
+            tsg[b] = g
+            bank = psum.tile([P, 4, P], F32, name="scale_bank", tag="scale_bank")
+            gs = g[:].rearrange("p (s j) -> p j s", j=4)
+            for j in range(4):
+                nc.tensor.transpose(bank[:, j, :], gs[:, j, :], ident[:])
+            col = keep.tile([P, 4, 1], F32, name=f"ts_col{b}")
+            nc.scalar.activation(out=col[:], in_=bank[:, :, 0:1], func=COPY)
+            ts_col[b] = col
+
+        def softmax(b):
+            k_codes = keep.tile([P, N], U32, name=f"k_codes{b}", align_bytes=64)
+            k_scales = keep.tile([P, N], U8, name=f"k_scales{b}", align_bytes=64)
+            nc.vector.quantize_mx(out=k_codes[:].bitcast(FP8X4), scales=k_scales[:], in_=kbf[b][:].rearrange("p n t -> p (n t)"))
+            score = psum.tile([P, N], F32, name="score", tag="score", bufs=2)
+            cols = slice(b * NQ, (b + 1) * NQ)
+            nc.tensor.matmul_mx(
+                out=score[:],
+                lhsT=q_codes[:, cols].bitcast(FP8X4),
+                lhsT_scale=q_scales[:, cols],
+                rhs=k_codes[:].bitcast(FP8X4),
+                rhs_scale=k_scales[:],
+                start=True,
+                stop=True,
+            )
+            a = keep.tile([P, 4, P], F32, name=f"a{b}")
+            nc.vector.tensor_tensor(
+                a[:],
+                score[:].rearrange("q (s j) -> q j s", j=4),
+                tsg[b][:].rearrange("q (s j) -> q j s", j=4),
+                MULT,
+            )
+            neg_m = keep.tile([P, 1], F32, name=f"neg_m{b}")
+            nc.vector.tensor_reduce(out=neg_m[:], in_=a[:].rearrange("q j s -> q (j s)"), axis=AXIS_X, op=MAX, negate=True)
+            p = keep.tile([P, 4, P], F32, name=f"p{b}")
+            l = keep.tile([P, 1], F32, name=f"l{b}")
+            nc.scalar.activation(out=p[:], in_=a[:], func=EXP, bias=neg_m[:], accum_out=l[:])
+            p_sb[b], l_sum[b] = p, l
+
+        v_codes, v_scales = {}, {}
+
+        def values(b):
+            vb = keep.tile([P, D, 4], BF16, name=f"vb{b}", align_bytes=64)
+            kf = kbf[b][:].rearrange("p n t -> p (n t)").bitcast(F32).rearrange("p (s j w) -> p w j s", j=4, w=2)
+            vview = vb[:].rearrange("s (p w e) j -> s w p e j", w=2, e=2)
+            for w in range(2):
+                bank = psum.tile([P, 4, P], F32, name="value_bank", tag="value_bank", bufs=3)
+                for j in range(4):
+                    nc.tensor.transpose(bank[:, j, :], kf[:, w, j, :], ident[:])
+                src = bank[:].rearrange("s j p -> s (j p)").bitcast(BF16).rearrange("s (j p e) -> s p e j", j=4, e=2)
+                nc.scalar.activation(out=vview[:, w], in_=src, func=COPY)
+            vc = keep.tile([P, D], U32, name=f"v_codes{b}", align_bytes=64)
+            vs = keep.tile([P, D], U8, name=f"v_scales{b}", align_bytes=64)
+            nc.vector.quantize_mx(out=vc[:].bitcast(FP8X4), scales=vs[:], in_=vb[:].rearrange("s d j -> s (d j)"))
+            v_codes[b], v_scales[b] = vc, vs
+
+        def output(b):
+            bank = psum.tile([P, 4, P], F32, name="weight_bank", tag="weight_bank")
+            for j in range(4):
+                nc.tensor.transpose(bank[:, j, :], p_sb[b][:, j, :], ident[:])
+            wb = keep.tile([P, NQ, 4], BF16, name=f"wb{b}", align_bytes=64)
+            nc.vector.tensor_tensor(
+                wb[:],
+                bank[:].rearrange("s j q -> s q j"),
+                ts_col[b][:].rearrange("s j o -> s o j").to_broadcast([P, NQ, 4]),
+                MULT,
+            )
+            wc = keep.tile([P, NQ], U32, name=f"w_codes{b}", align_bytes=64)
+            ws = keep.tile([P, NQ], U8, name=f"w_scales{b}", align_bytes=64)
+            nc.vector.quantize_mx(out=wc[:].bitcast(FP8X4), scales=ws[:], in_=wb[:].rearrange("s q j -> s (q j)"))
+            y = psum.tile([P, D], F32, name="y", tag="y")
+            nc.tensor.matmul_mx(
+                out=y[:],
+                lhsT=wc[:].bitcast(FP8X4),
+                lhsT_scale=ws[:],
+                rhs=v_codes[b][:].bitcast(FP8X4),
+                rhs_scale=v_scales[b][:],
+                start=True,
+                stop=True,
+            )
+            inv_l = keep.tile([P, 1], F32, name=f"inv_l{b}")
+            nc.vector.reciprocal(inv_l[:], l_sum[b][:])
+            o = keep.tile([P, D], F32, name=f"o{b}")
+            parts = 2 if b else 1
+            for i in range(parts):
+                d0, d1 = i * D // parts, (i + 1) * D // parts
+                nc.vector.scalar_tensor_tensor(out=o[:, d0:d1], in0=y[:, d0:d1], scalar=inv_l[:], in1=gate[b][:, d0:d1], op0=MULT, op1=MULT)
+                nc.sync.dma_start(out=out[b][:, d0:d1], in_=o[:, d0:d1])
+
+        gate = {}
+
+        def gates(b):
+            th = keep.tile([P, D], F32, name=f"th{b}")
+            nc.scalar.activation(out=th[:], in_=og_sb[:, b, :], func=TANH, scale=0.5)
+            sg = keep.tile([P, D], F32, name=f"sg{b}")
+            nc.gpsimd.tensor_scalar(sg[:], th[:], 0.5, 0.5, MULT, ADD)
+            g = keep.tile([P, D], F32, name=f"gate{b}")
+            nc.gpsimd.tensor_tensor(g[:], sg[:], ch_sb[:], MULT)
+            gate[b] = g
+
+        def queries(b):
+            nc.gpsimd.tensor_scalar(q_bf[:, b], q_raw[:, b].rearrange("p t q -> p q t"), 1.0, 0.0, MULT, ADD)
+            cols = slice(b * NQ, (b + 1) * NQ)
+            nc.vector.quantize_mx(out=q_codes[:, cols].bitcast(FP8X4), scales=q_scales[:, cols], in_=q_bf[:, b].rearrange("p q t -> p (q t)"))
+
+        gather_scales(0)
+        gather_latents(0)
+        queries(0)
+        softmax(0)
+        gather_latents(1)
+        gather_scales(1)
+        queries(1)
+        softmax(1)
+        values(0)
+        for b in range(B):
+            gates(b)
+        output(0)
+        values(1)
+        output(1)

@@ -8,6 +8,7 @@ FLOPS = 2 * 2 * 2 * 128 * 512 * 512
 F32 = mybir.dt.float32
 BF16 = mybir.dt.bfloat16
 U32 = mybir.dt.uint32
+I32 = mybir.dt.int32
 U16 = mybir.dt.uint16
 U8 = mybir.dt.uint8
 FP8X4 = mybir.dt.float8_e4m3fn_x4
@@ -27,7 +28,7 @@ SEG = T // B
 D = 512
 NQ = 128
 HALF = SEG // 2
-ON_VECTOR = {(0, 0, 1), (1, 1, 1)}
+S_SHARE = 384
 
 
 def tile_attend_x_mla_gate_seg_kernel(tc, qT, cT, ts, ch, og, offs, out):
@@ -43,11 +44,10 @@ def tile_attend_x_mla_gate_seg_kernel(tc, qT, cT, ts, ch, og, offs, out):
         c_rows = cT.rearrange("(p t) n -> p t n", t=4)
         raw = {}
 
-        def load_c(b, w, h):
-            piece = keep.tile([P, 2, HALF], F32, name=f"raw{b}{w}{h}")
-            n0 = b * SEG + h * HALF
-            nc.sync.dma_start(out=piece[:], in_=c_rows[:, 2 * w : 2 * w + 2, n0 : n0 + HALF])
-            raw[b, w, h] = piece
+        def load_c(b, w, n0, n1):
+            piece = keep.tile([P, 2, n1 - n0], F32, name=f"raw{b}{w}{n0}")
+            nc.sync.dma_start(out=piece[:], in_=c_rows[:, 2 * w : 2 * w + 2, n0:n1])
+            raw[b, w, n0] = piece
 
         scale_tab = keep.tile([P, T], F32, name="scale_tab")
         q_raw = keep.tile([P, B, 4, NQ], F32, name="q_raw")
@@ -61,15 +61,14 @@ def tile_attend_x_mla_gate_seg_kernel(tc, qT, cT, ts, ch, og, offs, out):
             nc.sync.dma_start(out=scale_tab[:, b * SEG : (b + 1) * SEG], in_=ts[:, b * SEG : (b + 1) * SEG])
 
         load_ts(0)
-        for w in range(2):
-            for h in range(2):
-                load_c(0, w, h)
+        load_c(0, 0, 0, SEG)
+        load_c(0, 1, 0, SEG)
         load_q(0)
-        load_c(1, 0, 0)
-        load_c(1, 0, 1)
+        load_c(1, 0, SEG, SEG + HALF)
+        load_c(1, 0, SEG + HALF, T)
         load_ts(1)
-        load_c(1, 1, 0)
-        load_c(1, 1, 1)
+        load_c(1, 1, SEG, SEG + HALF)
+        load_c(1, 1, SEG + HALF, T)
         load_q(1)
         nc.sync.dma_start(out=ch_sb[:], in_=ch)
         for b in range(B):
@@ -90,25 +89,38 @@ def tile_attend_x_mla_gate_seg_kernel(tc, qT, cT, ts, ch, og, offs, out):
         def words(tile):
             return tile[:].rearrange("p n e -> p (n e)").bitcast(U32)
 
-        kbf, tsg, p_sb, l_sum, ts_col = {}, {}, {}, {}, {}
+        kbf, planes, tsg, p_sb, l_sum, ts_col = {}, {}, {}, {}, {}, {}
+
+        def cast(engine, w, n0, n1, src):
+            dst = pairs[w][:, n0:n1, :]
+            src = src.rearrange("p e n -> p n e")
+            if engine == "vector":
+                nc.vector.tensor_copy(out=dst, in_=src)
+            else:
+                nc.scalar.activation(out=dst, in_=src, func=COPY)
 
         def gather_latents(b):
+            g = keep.tile([P, 2, N, 2], BF16, name=f"planes{b}", align_bytes=64)
+            planes[b] = g
             kb = keep.tile([P, N, 4], BF16, name=f"kb{b}", align_bytes=64)
             kbf[b] = kb
-            kw = kb[:].rearrange("p n t -> p (n t)").bitcast(U32).rearrange("p (n w) -> p w n", w=2)
+            gw = g[:].rearrange("p w n e -> p (w n e)").bitcast(U32).rearrange("p (w n) -> p w n", w=2)
             for w in range(2):
-                for h in range(2):
-                    n0 = b * SEG + h * HALF
-                    dst = pairs[w][:, n0 : n0 + HALF, :]
-                    rd = raw[b, w, h][:].rearrange("p e n -> p n e")
-                    if (b, w, h) in ON_VECTOR:
-                        nc.vector.tensor_copy(out=dst, in_=rd)
-                    else:
-                        nc.scalar.activation(out=dst, in_=rd, func=COPY)
+                if b == 0:
+                    piece = raw[0, w, 0]
+                    cast("scalar", w, 0, S_SHARE, piece[:, :, 0:S_SHARE])
+                    cast("vector", w, S_SHARE, SEG, piece[:, :, S_SHARE:SEG])
+                else:
+                    for n0 in (SEG, SEG + HALF):
+                        cast("scalar", w, n0, n0 + HALF, raw[1, w, n0][:])
                 window = words(pairs[w])
                 if b == 0:
                     window = window[:, 0:SEG]
-                nc.vector.tensor_copy(kw[:, w, :], window.indirect(offsets[:, b * (N // 16) : (b + 1) * (N // 16)]))
+                nc.vector.tensor_copy(gw[:, w, :], window.indirect(offsets[:, b * (N // 16) : (b + 1) * (N // 16)]))
+            nc.vector.tensor_copy(
+                out=kb[:].rearrange("p n t -> p (n t)").bitcast(I32).rearrange("p (n w) -> p n w", w=2),
+                in_=g[:].rearrange("p w n e -> p (w n e)").bitcast(I32).rearrange("p (w n) -> p n w", w=2),
+            )
 
         def gather_scales(b):
             g = keep.tile([P, N], F32, name=f"tsg{b}")
@@ -148,15 +160,17 @@ def tile_attend_x_mla_gate_seg_kernel(tc, qT, cT, ts, ch, og, offs, out):
             neg_m = keep.tile([P, 1], F32, name=f"neg_m{b}")
             nc.vector.tensor_reduce(out=neg_m[:], in_=a[:].rearrange("q j s -> q (j s)"), axis=AXIS_X, op=MAX, negate=True)
             p = keep.tile([P, 4, P], F32, name=f"p{b}")
-            l = keep.tile([P, 1], F32, name=f"l{b}")
-            nc.scalar.activation(out=p[:], in_=a[:], func=EXP, bias=neg_m[:], accum_out=l[:])
+            l = keep.tile([P, 2], F32, name=f"l{b}")
+            for h in range(2):
+                j2 = slice(2 * h, 2 * h + 2)
+                nc.scalar.activation(out=p[:, j2], in_=a[:, j2], func=EXP, bias=neg_m[:], accum_out=l[:, h : h + 1])
             p_sb[b], l_sum[b] = p, l
 
         v_codes, v_scales = {}, {}
 
         def values(b):
             vb = keep.tile([P, D, 4], BF16, name=f"vb{b}", align_bytes=64)
-            kf = kbf[b][:].rearrange("p n t -> p (n t)").bitcast(F32).rearrange("p (s j w) -> p w j s", j=4, w=2)
+            kf = planes[b][:].rearrange("p w n e -> p (w n e)").bitcast(F32).rearrange("p (w s j) -> p w j s", j=4, w=2)
             vview = vb[:].rearrange("s (p w e) j -> s w p e j", w=2, e=2)
             for w in range(2):
                 bank = psum.tile([P, 4, P], F32, name="value_bank", tag="value_bank", bufs=3)
@@ -194,7 +208,9 @@ def tile_attend_x_mla_gate_seg_kernel(tc, qT, cT, ts, ch, og, offs, out):
                 stop=True,
             )
             inv_l = keep.tile([P, 1], F32, name=f"inv_l{b}")
-            nc.vector.reciprocal(inv_l[:], l_sum[b][:])
+            l = keep.tile([P, 1], F32, name=f"l_all{b}")
+            nc.gpsimd.tensor_tensor(l[:], l_sum[b][:, 0:1], l_sum[b][:, 1:2], ADD)
+            nc.vector.reciprocal(inv_l[:], l[:])
             o = keep.tile([P, D], F32, name=f"o{b}")
             parts = 2 if b else 1
             for i in range(parts):

@@ -28,7 +28,7 @@ SEG = T // B
 D = 512
 NQ = 128
 HALF = SEG // 2
-S_SHARE = 384
+LIST = N // 16
 
 
 def tile_attend_x_mla_gate_seg_kernel(tc, qT, cT, ts, ch, og, offs, out):
@@ -38,213 +38,266 @@ def tile_attend_x_mla_gate_seg_kernel(tc, qT, cT, ts, ch, og, offs, out):
         keep = ctx.enter_context(tc.tile_pool(name="keep", bufs=1))
         psum = ctx.enter_context(tc.psum_pool(name="psum", bufs=1))
 
-        offsets = lists.tile([P, B * N // 16], U16, name="offsets")
+        offsets = lists.tile([P, B * LIST], U16, name="offsets")
         nc.sync.dma_start(offsets[:], offs)
 
-        c_rows = cT.rearrange("(p t) n -> p t n", t=4)
-        raw = {}
+        def each(shape, dtype, name):
+            return [keep.tile(shape, dtype, name=f"{name}{b}", align_bytes=64) for b in range(B)]
 
-        def load_c(b, w, n0, n1):
-            piece = keep.tile([P, 2, n1 - n0], F32, name=f"raw{b}{w}{n0}")
-            nc.sync.dma_start(out=piece[:], in_=c_rows[:, 2 * w : 2 * w + 2, n0:n1])
-            raw[b, w, n0] = piece
-
+        raw = {(b, w, h): keep.tile([P, 2, HALF], F32, name=f"raw{b}{w}{h}") for b in range(B) for w in range(2) for h in range(2)}
         scale_tab = keep.tile([P, T], F32, name="scale_tab")
-        q_raw = keep.tile([P, B, 4, NQ], F32, name="q_raw")
+        q_raw = each([P, 4, NQ], F32, "q_raw")
         ch_sb = keep.tile([P, D], F32, name="ch_sb")
-        og_sb = keep.tile([P, B, D], F32, name="og_sb")
+        og_sb = each([P, D], F32, "og_sb")
+        pairs = [keep.tile([P, T, 2], BF16, name=f"pairs{w}", align_bytes=64) for w in range(2)]
+        kb = each([P, N, 4], BF16, "kb")
+        k_codes, k_scales = each([P, N], U32, "k_codes"), each([P, N], U8, "k_scales")
+        q_bf = each([P, NQ, 4], BF16, "q_bf")
+        q_codes, q_scales = each([P, NQ], U32, "q_codes"), each([P, NQ], U8, "q_scales")
+        tsg = each([P, N], F32, "tsg")
+        ts_col = each([P, 4, 1], F32, "ts_col")
+        a = each([P, 4, P], F32, "a")
+        neg_m = each([P, 1], F32, "neg_m")
+        p = each([P, 4, P], F32, "p")
+        l_half = each([P, 2], F32, "l_half")
+        l_sum = each([P, 1], F32, "l_sum")
+        inv_l = each([P, 1], F32, "inv_l")
+        vb = each([P, D, 4], BF16, "vb")
+        v_codes, v_scales = each([P, D], U32, "v_codes"), each([P, D], U8, "v_scales")
+        wb = each([P, NQ, 4], BF16, "wb")
+        w_codes, w_scales = each([P, NQ], U32, "w_codes"), each([P, NQ], U8, "w_scales")
+        th = each([P, D], F32, "th")
+        sg = each([P, D], F32, "sg")
+        gate = each([P, D], F32, "gate")
+        o = each([P, D], F32, "o")
+        bank = {}
 
-        def load_q(b):
-            nc.sync.dma_start(out=q_raw[:, b], in_=qT[b].rearrange("(p t) q -> p t q", t=4))
-
-        def load_ts(b):
-            nc.sync.dma_start(out=scale_tab[:, b * SEG : (b + 1) * SEG], in_=ts[:, b * SEG : (b + 1) * SEG])
-
-        load_ts(0)
-        load_c(0, 0, 0, SEG)
-        load_c(0, 1, 0, SEG)
-        load_q(0)
-        load_c(1, 0, SEG, SEG + HALF)
-        load_c(1, 0, SEG + HALF, T)
-        load_ts(1)
-        load_c(1, 1, SEG, SEG + HALF)
-        load_c(1, 1, SEG + HALF, T)
-        load_q(1)
-        nc.sync.dma_start(out=ch_sb[:], in_=ch)
-        for b in range(B):
-            nc.sync.dma_start(out=og_sb[:, b, :], in_=og[b])
-
-        warm = keep.tile([P, 1], F32, name="warm")
-        nc.vector.memset(warm[:], 0.0)
-        warmed = keep.tile([P, 1], F32, name="warmed")
-        nc.scalar.activation(out=warmed[:], in_=warm[:], func=EXP)
         ident = keep.tile([P, P], F32, name="ident")
         make_identity(nc, ident[:])
+        warm = keep.tile([P, 1], F32, name="warm")
+        warmed = keep.tile([P, 1], F32, name="warmed")
 
-        pairs = [keep.tile([P, T, 2], BF16, name=f"pairs{w}", align_bytes=64) for w in range(2)]
-        q_bf = keep.tile([P, B, NQ, 4], BF16, name="q_bf", align_bytes=64)
-        q_codes = keep.tile([P, B * NQ], U32, name="q_codes", align_bytes=64)
-        q_scales = keep.tile([P, B * NQ], U8, name="q_scales", align_bytes=64)
+        def preload_exp():
+            nc.vector.memset(warm[:], 0.0)
+            nc.scalar.activation(out=warmed[:], in_=warm[:], func=EXP)
 
-        def words(tile):
-            return tile[:].rearrange("p n e -> p (n e)").bitcast(U32)
+        def load_pair(b, w, h):
+            n0 = b * SEG + h * HALF
+            nc.sync.dma_start(out=raw[b, w, h][:], in_=cT.rearrange("(p t) n -> p t n", t=4)[:, 2 * w : 2 * w + 2, n0 : n0 + HALF])
 
-        kbf, planes, tsg, p_sb, l_sum, ts_col = {}, {}, {}, {}, {}, {}
+        def load_scales(b):
+            nc.sync.dma_start(out=scale_tab[:, b * SEG : (b + 1) * SEG], in_=ts[:, b * SEG : (b + 1) * SEG])
 
-        def cast(engine, w, n0, n1, src):
-            dst = pairs[w][:, n0:n1, :]
-            src = src.rearrange("p e n -> p n e")
-            if engine == "vector":
-                nc.vector.tensor_copy(out=dst, in_=src)
-            else:
+        def load_queries(b):
+            nc.sync.dma_start(out=q_raw[b][:], in_=qT[b].rearrange("(p t) q -> p t q", t=4))
+
+        def load_channels():
+            nc.sync.dma_start(out=ch_sb[:], in_=ch)
+
+        def load_gate(b):
+            nc.sync.dma_start(out=og_sb[b][:], in_=og[b])
+
+        def cast(engine, b, w, h):
+            n0 = b * SEG + h * HALF
+            dst = pairs[w][:, n0 : n0 + HALF, :]
+            src = raw[b, w, h][:].rearrange("p e n -> p n e")
+            if engine is nc.scalar:
                 nc.scalar.activation(out=dst, in_=src, func=COPY)
+            else:
+                nc.vector.tensor_copy(out=dst, in_=src)
 
-        def gather_latents(b):
-            g = keep.tile([P, 2, N, 2], BF16, name=f"planes{b}", align_bytes=64)
-            planes[b] = g
-            kb = keep.tile([P, N, 4], BF16, name=f"kb{b}", align_bytes=64)
-            kbf[b] = kb
-            gw = g[:].rearrange("p w n e -> p (w n e)").bitcast(U32).rearrange("p (w n) -> p w n", w=2)
-            for w in range(2):
-                if b == 0:
-                    piece = raw[0, w, 0]
-                    cast("scalar", w, 0, S_SHARE, piece[:, :, 0:S_SHARE])
-                    cast("vector", w, S_SHARE, SEG, piece[:, :, S_SHARE:SEG])
-                else:
-                    for n0 in (SEG, SEG + HALF):
-                        cast("scalar", w, n0, n0 + HALF, raw[1, w, n0][:])
-                window = words(pairs[w])
-                if b == 0:
-                    window = window[:, 0:SEG]
-                nc.vector.tensor_copy(gw[:, w, :], window.indirect(offsets[:, b * (N // 16) : (b + 1) * (N // 16)]))
-            nc.vector.tensor_copy(
-                out=kb[:].rearrange("p n t -> p (n t)").bitcast(I32).rearrange("p (n w) -> p n w", w=2),
-                in_=g[:].rearrange("p w n e -> p (w n e)").bitcast(I32).rearrange("p (w n) -> p n w", w=2),
-            )
+        def gather_pair(b, w):
+            window = pairs[w][:].rearrange("p n e -> p (n e)").bitcast(U32)
+            if b == 0:
+                window = window[:, 0:SEG]
+            dst = kb[b][:].rearrange("p n t -> p (n t)").bitcast(U32).rearrange("p (n w) -> p w n", w=2)[:, w, :]
+            nc.vector.tensor_copy(dst, window.indirect(offsets[:, b * LIST : (b + 1) * LIST]))
 
         def gather_scales(b):
-            g = keep.tile([P, N], F32, name=f"tsg{b}")
             window = scale_tab[:] if b else scale_tab[:, 0:SEG]
-            nc.vector.tensor_copy(g[:], window.indirect(offsets[:, b * (N // 16) : (b + 1) * (N // 16)]))
-            tsg[b] = g
-            bank = psum.tile([P, 4, P], F32, name="scale_bank", tag="scale_bank")
-            gs = g[:].rearrange("p (s j) -> p j s", j=4)
-            for j in range(4):
-                nc.tensor.transpose(bank[:, j, :], gs[:, j, :], ident[:])
-            col = keep.tile([P, 4, 1], F32, name=f"ts_col{b}")
-            nc.scalar.activation(out=col[:], in_=bank[:, :, 0:1], func=COPY)
-            ts_col[b] = col
+            nc.vector.tensor_copy(tsg[b][:], window.indirect(offsets[:, b * LIST : (b + 1) * LIST]))
 
-        def softmax(b):
-            k_codes = keep.tile([P, N], U32, name=f"k_codes{b}", align_bytes=64)
-            k_scales = keep.tile([P, N], U8, name=f"k_scales{b}", align_bytes=64)
-            nc.vector.quantize_mx(out=k_codes[:].bitcast(FP8X4), scales=k_scales[:], in_=kbf[b][:].rearrange("p n t -> p (n t)"))
-            score = psum.tile([P, N], F32, name="score", tag="score", bufs=2)
-            cols = slice(b * NQ, (b + 1) * NQ)
+        def turn_scales(b):
+            bank["ts", b] = psum.tile([P, 4, P], F32, name="scale_bank", tag="scale_bank")
+            for j in range(4):
+                nc.tensor.transpose(bank["ts", b][:, j, :], tsg[b][:].rearrange("q (s j) -> q j s", j=4)[:, j, :], ident[:])
+
+        def scale_column(b):
+            nc.scalar.activation(out=ts_col[b][:], in_=bank["ts", b][:, :, 0:1], func=COPY)
+
+        def cast_queries(b):
+            nc.gpsimd.tensor_scalar(q_bf[b][:], q_raw[b][:].rearrange("p t q -> p q t"), 1.0, 0.0, MULT, ADD)
+
+        def quantise(codes, scales, src):
+            nc.vector.quantize_mx(out=codes[:].bitcast(FP8X4), scales=scales[:], in_=src[:].rearrange("p n t -> p (n t)"))
+
+        def quantise_queries(b):
+            quantise(q_codes[b], q_scales[b], q_bf[b])
+
+        def quantise_keys(b):
+            quantise(k_codes[b], k_scales[b], kb[b])
+
+        def quantise_values(b):
+            quantise(v_codes[b], v_scales[b], vb[b])
+
+        def quantise_weights(b):
+            quantise(w_codes[b], w_scales[b], wb[b])
+
+        def scores(b):
+            bank["score", b] = psum.tile([P, N], F32, name="score", tag="score", bufs=2)
             nc.tensor.matmul_mx(
-                out=score[:],
-                lhsT=q_codes[:, cols].bitcast(FP8X4),
-                lhsT_scale=q_scales[:, cols],
-                rhs=k_codes[:].bitcast(FP8X4),
-                rhs_scale=k_scales[:],
+                out=bank["score", b][:],
+                lhsT=q_codes[b][:].bitcast(FP8X4),
+                lhsT_scale=q_scales[b][:],
+                rhs=k_codes[b][:].bitcast(FP8X4),
+                rhs_scale=k_scales[b][:],
                 start=True,
                 stop=True,
             )
-            a = keep.tile([P, 4, P], F32, name=f"a{b}")
+
+        def scale_scores(b):
             nc.vector.tensor_tensor(
-                a[:],
-                score[:].rearrange("q (s j) -> q j s", j=4),
+                a[b][:],
+                bank["score", b][:].rearrange("q (s j) -> q j s", j=4),
                 tsg[b][:].rearrange("q (s j) -> q j s", j=4),
                 MULT,
             )
-            neg_m = keep.tile([P, 1], F32, name=f"neg_m{b}")
-            nc.vector.tensor_reduce(out=neg_m[:], in_=a[:].rearrange("q j s -> q (j s)"), axis=AXIS_X, op=MAX, negate=True)
-            p = keep.tile([P, 4, P], F32, name=f"p{b}")
-            l = keep.tile([P, 2], F32, name=f"l{b}")
+
+        def maximum(b):
+            nc.vector.tensor_reduce(out=neg_m[b][:], in_=a[b][:].rearrange("q j s -> q (j s)"), axis=AXIS_X, op=MAX, negate=True)
+
+        def exponentials(b):
             for h in range(2):
                 j2 = slice(2 * h, 2 * h + 2)
-                nc.scalar.activation(out=p[:, j2], in_=a[:, j2], func=EXP, bias=neg_m[:], accum_out=l[:, h : h + 1])
-            p_sb[b], l_sum[b] = p, l
+                nc.scalar.activation(out=p[b][:, j2], in_=a[b][:, j2], func=EXP, bias=neg_m[b][:], accum_out=l_half[b][:, h : h + 1])
 
-        v_codes, v_scales = {}, {}
+        def invert_sums(b):
+            nc.gpsimd.tensor_tensor(l_sum[b][:], l_half[b][:, 0:1], l_half[b][:, 1:2], ADD)
+            nc.vector.reciprocal(inv_l[b][:], l_sum[b][:])
 
-        def values(b):
-            vb = keep.tile([P, D, 4], BF16, name=f"vb{b}", align_bytes=64)
-            kf = planes[b][:].rearrange("p w n e -> p (w n e)").bitcast(F32).rearrange("p (w s j) -> p w j s", j=4, w=2)
-            vview = vb[:].rearrange("s (p w e) j -> s w p e j", w=2, e=2)
-            for w in range(2):
-                bank = psum.tile([P, 4, P], F32, name="value_bank", tag="value_bank", bufs=3)
-                for j in range(4):
-                    nc.tensor.transpose(bank[:, j, :], kf[:, w, j, :], ident[:])
-                src = bank[:].rearrange("s j p -> s (j p)").bitcast(BF16).rearrange("s (j p e) -> s p e j", j=4, e=2)
-                nc.scalar.activation(out=vview[:, w], in_=src, func=COPY)
-            vc = keep.tile([P, D], U32, name=f"v_codes{b}", align_bytes=64)
-            vs = keep.tile([P, D], U8, name=f"v_scales{b}", align_bytes=64)
-            nc.vector.quantize_mx(out=vc[:].bitcast(FP8X4), scales=vs[:], in_=vb[:].rearrange("s d j -> s (d j)"))
-            v_codes[b], v_scales[b] = vc, vs
-
-        def output(b):
-            bank = psum.tile([P, 4, P], F32, name="weight_bank", tag="weight_bank")
+        def turn_values(b, w):
+            bank["v", b, w] = psum.tile([P, 4, P], F32, name="value_bank", tag="value_bank", bufs=3)
+            words = kb[b][:].rearrange("p n t -> p (n t)").bitcast(F32).rearrange("p (s j w) -> p w j s", j=4, w=2)
             for j in range(4):
-                nc.tensor.transpose(bank[:, j, :], p_sb[b][:, j, :], ident[:])
-            wb = keep.tile([P, NQ, 4], BF16, name=f"wb{b}", align_bytes=64)
+                nc.tensor.transpose(bank["v", b, w][:, j, :], words[:, w, j, :], ident[:])
+
+        def copy_values(b, w):
+            src = bank["v", b, w][:].rearrange("s j p -> s (j p)").bitcast(BF16).rearrange("s (j p e) -> s p e j", j=4, e=2)
+            nc.scalar.activation(out=vb[b][:].rearrange("s (p w e) j -> s w p e j", w=2, e=2)[:, w], in_=src, func=COPY)
+
+        def turn_weights(b):
+            bank["w", b] = psum.tile([P, 4, P], F32, name="weight_bank", tag="weight_bank")
+            for j in range(4):
+                nc.tensor.transpose(bank["w", b][:, j, :], p[b][:, j, :], ident[:])
+
+        def scale_weights(b):
             nc.vector.tensor_tensor(
-                wb[:],
-                bank[:].rearrange("s j q -> s q j"),
+                wb[b][:],
+                bank["w", b][:].rearrange("s j q -> s q j"),
                 ts_col[b][:].rearrange("s j o -> s o j").to_broadcast([P, NQ, 4]),
                 MULT,
             )
-            wc = keep.tile([P, NQ], U32, name=f"w_codes{b}", align_bytes=64)
-            ws = keep.tile([P, NQ], U8, name=f"w_scales{b}", align_bytes=64)
-            nc.vector.quantize_mx(out=wc[:].bitcast(FP8X4), scales=ws[:], in_=wb[:].rearrange("s q j -> s (q j)"))
-            y = psum.tile([P, D], F32, name="y", tag="y")
+
+        def products(b):
+            bank["y", b] = psum.tile([P, D], F32, name="y", tag="y")
             nc.tensor.matmul_mx(
-                out=y[:],
-                lhsT=wc[:].bitcast(FP8X4),
-                lhsT_scale=ws[:],
+                out=bank["y", b][:],
+                lhsT=w_codes[b][:].bitcast(FP8X4),
+                lhsT_scale=w_scales[b][:],
                 rhs=v_codes[b][:].bitcast(FP8X4),
                 rhs_scale=v_scales[b][:],
                 start=True,
                 stop=True,
             )
-            inv_l = keep.tile([P, 1], F32, name=f"inv_l{b}")
-            l = keep.tile([P, 1], F32, name=f"l_all{b}")
-            nc.gpsimd.tensor_tensor(l[:], l_sum[b][:, 0:1], l_sum[b][:, 1:2], ADD)
-            nc.vector.reciprocal(inv_l[:], l[:])
-            o = keep.tile([P, D], F32, name=f"o{b}")
-            parts = 2 if b else 1
-            for i in range(parts):
-                d0, d1 = i * D // parts, (i + 1) * D // parts
-                nc.vector.scalar_tensor_tensor(out=o[:, d0:d1], in0=y[:, d0:d1], scalar=inv_l[:], in1=gate[b][:, d0:d1], op0=MULT, op1=MULT)
-                nc.sync.dma_start(out=out[b][:, d0:d1], in_=o[:, d0:d1])
 
-        gate = {}
+        def gate_tanh(b):
+            nc.scalar.activation(out=th[b][:], in_=og_sb[b][:], func=TANH, scale=0.5)
 
-        def gates(b):
-            th = keep.tile([P, D], F32, name=f"th{b}")
-            nc.scalar.activation(out=th[:], in_=og_sb[:, b, :], func=TANH, scale=0.5)
-            sg = keep.tile([P, D], F32, name=f"sg{b}")
-            nc.gpsimd.tensor_scalar(sg[:], th[:], 0.5, 0.5, MULT, ADD)
-            g = keep.tile([P, D], F32, name=f"gate{b}")
-            nc.gpsimd.tensor_tensor(g[:], sg[:], ch_sb[:], MULT)
-            gate[b] = g
+        def gate_sigmoid(b):
+            nc.gpsimd.tensor_scalar(sg[b][:], th[b][:], 0.5, 0.5, MULT, ADD)
 
-        def queries(b):
-            nc.gpsimd.tensor_scalar(q_bf[:, b], q_raw[:, b].rearrange("p t q -> p q t"), 1.0, 0.0, MULT, ADD)
-            cols = slice(b * NQ, (b + 1) * NQ)
-            nc.vector.quantize_mx(out=q_codes[:, cols].bitcast(FP8X4), scales=q_scales[:, cols], in_=q_bf[:, b].rearrange("p q t -> p (q t)"))
+        def gate_channels(b):
+            nc.gpsimd.tensor_tensor(gate[b][:], sg[b][:], ch_sb[:], MULT)
 
+        def finish(b):
+            for i in range(2):
+                d = slice(i * D // 2, (i + 1) * D // 2)
+                nc.vector.scalar_tensor_tensor(out=o[b][:, d], in0=bank["y", b][:, d], scalar=inv_l[b][:], in1=gate[b][:, d], op0=MULT, op1=MULT)
+                nc.sync.dma_start(out=out[b][:, d], in_=o[b][:, d])
+
+        load_pair(0, 0, 0)
+        load_pair(0, 0, 1)
+        load_scales(0)
+        load_pair(0, 1, 0)
+        load_pair(0, 1, 1)
+        load_queries(0)
+        load_pair(1, 0, 0)
+        load_pair(1, 0, 1)
+        load_pair(1, 1, 0)
+        load_pair(1, 1, 1)
+        load_queries(1)
+        load_scales(1)
+        load_channels()
+        load_gate(0)
+        load_gate(1)
+        preload_exp()
+        cast(nc.scalar, 0, 0, 0)
+        cast(nc.vector, 0, 0, 1)
+        gather_pair(0, 0)
         gather_scales(0)
-        gather_latents(0)
-        queries(0)
-        softmax(0)
-        gather_latents(1)
+        turn_scales(0)
+        turn_values(0, 0)
+        cast(nc.scalar, 0, 1, 0)
+        cast(nc.vector, 0, 1, 1)
+        gather_pair(0, 1)
+        cast_queries(0)
+        cast(nc.scalar, 1, 0, 0)
+        quantise_queries(0)
+        cast(nc.scalar, 1, 0, 1)
+        quantise_keys(0)
+        scores(0)
+        gather_pair(1, 0)
+        turn_values(0, 1)
+        cast(nc.scalar, 1, 1, 0)
+        scale_scores(0)
+        turn_values(1, 0)
+        cast(nc.scalar, 1, 1, 1)
+        gather_pair(1, 1)
+        copy_values(0, 0)
+        copy_values(0, 1)
+        scale_column(0)
+        cast_queries(1)
+        turn_values(1, 1)
+        quantise_queries(1)
+        maximum(0)
+        quantise_keys(1)
+        exponentials(0)
+        gate_tanh(0)
+        gate_sigmoid(0)
+        copy_values(1, 0)
+        scores(1)
+        gate_channels(0)
+        turn_weights(0)
         gather_scales(1)
-        queries(1)
-        softmax(1)
-        values(0)
-        for b in range(B):
-            gates(b)
-        output(0)
-        values(1)
-        output(1)
+        invert_sums(0)
+        scale_scores(1)
+        turn_scales(1)
+        maximum(1)
+        scale_weights(0)
+        quantise_values(0)
+        quantise_weights(0)
+        copy_values(1, 1)
+        quantise_values(1)
+        exponentials(1)
+        invert_sums(1)
+        scale_column(1)
+        gate_tanh(1)
+        turn_weights(1)
+        scale_weights(1)
+        products(0)
+        gate_sigmoid(1)
+        gate_channels(1)
+        finish(0)
+        quantise_weights(1)
+        products(1)
+        finish(1)

@@ -29,6 +29,7 @@ D = 512
 NQ = 128
 HALF = SEG // 2
 LIST = N // 16
+ALL, LEFT, RIGHT = slice(0, N), slice(0, N // 2), slice(N // 2, N)
 
 
 def tile_attend_x_mla_gate_seg_kernel(tc, qT, cT, ts, ch, og, offs, out):
@@ -39,7 +40,6 @@ def tile_attend_x_mla_gate_seg_kernel(tc, qT, cT, ts, ch, og, offs, out):
         psum = ctx.enter_context(tc.psum_pool(name="psum", bufs=1))
 
         offsets = lists.tile([P, B * LIST], U16, name="offsets")
-        nc.sync.dma_start(offsets[:], offs)
 
         def each(shape, dtype, name):
             return [keep.tile(shape, dtype, name=f"{name}{b}", align_bytes=64) for b in range(B)]
@@ -67,7 +67,6 @@ def tile_attend_x_mla_gate_seg_kernel(tc, qT, cT, ts, ch, og, offs, out):
         wb = each([P, NQ, 4], BF16, "wb")
         w_codes, w_scales = each([P, NQ], U32, "w_codes"), each([P, NQ], U8, "w_scales")
         th = each([P, D], F32, "th")
-        sg = each([P, D], F32, "sg")
         gate = each([P, D], F32, "gate")
         o = each([P, D], F32, "o")
         bank = {}
@@ -110,17 +109,19 @@ def tile_attend_x_mla_gate_seg_kernel(tc, qT, cT, ts, ch, og, offs, out):
             window = pairs[w][:].rearrange("p n e -> p (n e)").bitcast(U32)
             if b == 0:
                 window = window[:, 0:SEG]
-            dst = kb[b][:].rearrange("p n t -> p (n t)").bitcast(U32).rearrange("p (n w) -> p w n", w=2)[:, w, :]
+            dst = kb[b][:].rearrange("p n t -> p (n t)").bitcast(U32).rearrange("p (j s w) -> p w s j", j=4, w=2)[:, w]
             nc.vector.tensor_copy(dst, window.indirect(offsets[:, b * LIST : (b + 1) * LIST]))
 
         def gather_scales(b):
-            window = scale_tab[:] if b else scale_tab[:, 0:SEG]
-            nc.vector.tensor_copy(tsg[b][:], window.indirect(offsets[:, b * LIST : (b + 1) * LIST]))
+            window = scale_tab[:].bitcast(U32)
+            if b == 0:
+                window = window[:, 0:SEG]
+            nc.vector.tensor_copy(tsg[b][:].bitcast(U32).rearrange("p (j s) -> p s j", j=4), window.indirect(offsets[:, b * LIST : (b + 1) * LIST]))
 
         def turn_scales(b):
             bank["ts", b] = psum.tile([P, 4, P], F32, name="scale_bank", tag="scale_bank")
             for j in range(4):
-                nc.tensor.transpose(bank["ts", b][:, j, :], tsg[b][:].rearrange("q (s j) -> q j s", j=4)[:, j, :], ident[:])
+                nc.tensor.transpose(bank["ts", b][:, j, :], tsg[b][:, j * P : (j + 1) * P], ident[:])
 
         def scale_column(b):
             nc.scalar.activation(out=ts_col[b][:], in_=bank["ts", b][:, :, 0:1], func=COPY)
@@ -134,8 +135,12 @@ def tile_attend_x_mla_gate_seg_kernel(tc, qT, cT, ts, ch, og, offs, out):
         def quantise_queries(b):
             quantise(q_codes[b], q_scales[b], q_bf[b])
 
-        def quantise_keys(b):
-            quantise(k_codes[b], k_scales[b], kb[b])
+        def quantise_keys(b, cols):
+            nc.vector.quantize_mx(
+                out=k_codes[b][:, cols].bitcast(FP8X4),
+                scales=k_scales[b][:, cols],
+                in_=kb[b][:, cols, :].rearrange("p n t -> p (n t)"),
+            )
 
         def quantise_values(b):
             quantise(v_codes[b], v_scales[b], vb[b])
@@ -143,25 +148,22 @@ def tile_attend_x_mla_gate_seg_kernel(tc, qT, cT, ts, ch, og, offs, out):
         def quantise_weights(b):
             quantise(w_codes[b], w_scales[b], wb[b])
 
-        def scores(b):
-            bank["score", b] = psum.tile([P, N], F32, name="score", tag="score", bufs=2)
+        def scores(b, cols):
+            tile = psum.tile([P, cols.stop - cols.start], F32, name="result", tag="result", bufs=3)
+            bank["score", b, cols.start] = tile
             nc.tensor.matmul_mx(
-                out=bank["score", b][:],
+                out=tile[:],
                 lhsT=q_codes[b][:].bitcast(FP8X4),
                 lhsT_scale=q_scales[b][:],
-                rhs=k_codes[b][:].bitcast(FP8X4),
-                rhs_scale=k_scales[b][:],
+                rhs=k_codes[b][:, cols].bitcast(FP8X4),
+                rhs_scale=k_scales[b][:, cols],
                 start=True,
                 stop=True,
             )
 
-        def scale_scores(b):
-            nc.vector.tensor_tensor(
-                a[b][:],
-                bank["score", b][:].rearrange("q (s j) -> q j s", j=4),
-                tsg[b][:].rearrange("q (s j) -> q j s", j=4),
-                MULT,
-            )
+        def scale_scores(b, cols):
+            flat = a[b][:].rearrange("q j s -> q (j s)")
+            nc.vector.tensor_tensor(flat[:, cols], bank["score", b, cols.start][:], tsg[b][:, cols], MULT)
 
         def maximum(b):
             nc.vector.tensor_reduce(out=neg_m[b][:], in_=a[b][:].rearrange("q j s -> q (j s)"), axis=AXIS_X, op=MAX, negate=True)
@@ -172,12 +174,12 @@ def tile_attend_x_mla_gate_seg_kernel(tc, qT, cT, ts, ch, og, offs, out):
                 nc.scalar.activation(out=p[b][:, j2], in_=a[b][:, j2], func=EXP, bias=neg_m[b][:], accum_out=l_half[b][:, h : h + 1])
 
         def invert_sums(b):
-            nc.gpsimd.tensor_tensor(l_sum[b][:], l_half[b][:, 0:1], l_half[b][:, 1:2], ADD)
+            nc.gpsimd.tensor_scalar(l_sum[b][:], l_half[b][:, 0:1], l_half[b][:, 1:2], 2.0, ADD, MULT)
             nc.vector.reciprocal(inv_l[b][:], l_sum[b][:])
 
         def turn_values(b, w):
             bank["v", b, w] = psum.tile([P, 4, P], F32, name="value_bank", tag="value_bank", bufs=3)
-            words = kb[b][:].rearrange("p n t -> p (n t)").bitcast(F32).rearrange("p (s j w) -> p w j s", j=4, w=2)
+            words = kb[b][:].rearrange("p n t -> p (n t)").bitcast(F32).rearrange("p (j s w) -> p w j s", j=4, w=2)
             for j in range(4):
                 nc.tensor.transpose(bank["v", b, w][:, j, :], words[:, w, j, :], ident[:])
 
@@ -198,14 +200,15 @@ def tile_attend_x_mla_gate_seg_kernel(tc, qT, cT, ts, ch, og, offs, out):
                 MULT,
             )
 
-        def products(b):
-            bank["y", b] = psum.tile([P, D], F32, name="y", tag="y")
+        def products(b, cols):
+            tile = psum.tile([P, cols.stop - cols.start], F32, name="result", tag="result", bufs=3)
+            bank["y", b, cols.start] = tile
             nc.tensor.matmul_mx(
-                out=bank["y", b][:],
+                out=tile[:],
                 lhsT=w_codes[b][:].bitcast(FP8X4),
                 lhsT_scale=w_scales[b][:],
-                rhs=v_codes[b][:].bitcast(FP8X4),
-                rhs_scale=v_scales[b][:],
+                rhs=v_codes[b][:, cols].bitcast(FP8X4),
+                rhs_scale=v_scales[b][:, cols],
                 start=True,
                 stop=True,
             )
@@ -213,26 +216,23 @@ def tile_attend_x_mla_gate_seg_kernel(tc, qT, cT, ts, ch, og, offs, out):
         def gate_tanh(b):
             nc.scalar.activation(out=th[b][:], in_=og_sb[b][:], func=TANH, scale=0.5)
 
-        def gate_sigmoid(b):
-            nc.gpsimd.tensor_scalar(sg[b][:], th[b][:], 0.5, 0.5, MULT, ADD)
-
         def gate_channels(b):
-            nc.gpsimd.tensor_tensor(gate[b][:], sg[b][:], ch_sb[:], MULT)
+            nc.vector.scalar_tensor_tensor(out=gate[b][:], in0=th[b][:], scalar=1.0, in1=ch_sb[:], op0=ADD, op1=MULT)
 
-        def finish(b):
-            for i in range(2):
-                d = slice(i * D // 2, (i + 1) * D // 2)
-                nc.vector.scalar_tensor_tensor(out=o[b][:, d], in0=bank["y", b][:, d], scalar=inv_l[b][:], in1=gate[b][:, d], op0=MULT, op1=MULT)
-                nc.sync.dma_start(out=out[b][:, d], in_=o[b][:, d])
+        def finish(b, cols):
+            y = bank["y", b, cols.start]
+            nc.vector.scalar_tensor_tensor(out=o[b][:, cols], in0=y[:], scalar=inv_l[b][:], in1=gate[b][:, cols], op0=MULT, op1=MULT)
+            nc.sync.dma_start(out=out[b][:, cols], in_=o[b][:, cols])
 
         load_pair(0, 0, 0)
         load_pair(0, 0, 1)
-        load_scales(0)
+        nc.sync.dma_start(offsets[:], offs)
         load_pair(0, 1, 0)
         load_pair(0, 1, 1)
         load_queries(0)
         load_pair(1, 0, 0)
         load_pair(1, 0, 1)
+        load_scales(0)
         load_pair(1, 1, 0)
         load_pair(1, 1, 1)
         load_queries(1)
@@ -243,61 +243,64 @@ def tile_attend_x_mla_gate_seg_kernel(tc, qT, cT, ts, ch, og, offs, out):
         preload_exp()
         cast(nc.scalar, 0, 0, 0)
         cast(nc.vector, 0, 0, 1)
-        gather_pair(0, 0)
-        gather_scales(0)
-        turn_scales(0)
-        turn_values(0, 0)
         cast(nc.scalar, 0, 1, 0)
-        cast(nc.vector, 0, 1, 1)
-        gather_pair(0, 1)
+        gather_pair(0, 0)
         cast_queries(0)
-        cast(nc.scalar, 1, 0, 0)
+        cast(nc.vector, 0, 1, 1)
+        turn_values(0, 0)
+        gather_pair(0, 1)
         quantise_queries(0)
-        cast(nc.scalar, 1, 0, 1)
-        quantise_keys(0)
-        scores(0)
-        gather_pair(1, 0)
+        quantise_keys(0, ALL)
+        gather_scales(0)
+        cast(nc.scalar, 1, 0, 0)
+        scores(0, ALL)
         turn_values(0, 1)
-        cast(nc.scalar, 1, 1, 0)
-        scale_scores(0)
-        turn_values(1, 0)
-        cast(nc.scalar, 1, 1, 1)
-        gather_pair(1, 1)
-        copy_values(0, 0)
-        copy_values(0, 1)
-        scale_column(0)
         cast_queries(1)
-        turn_values(1, 1)
-        quantise_queries(1)
+        turn_scales(0)
+        copy_values(0, 0)
+        cast(nc.scalar, 1, 0, 1)
+        scale_scores(0, ALL)
+        cast(nc.scalar, 1, 1, 0)
+        cast(nc.scalar, 1, 1, 1)
+        gather_pair(1, 0)
         maximum(0)
-        quantise_keys(1)
+        turn_values(1, 0)
+        gather_pair(1, 1)
         exponentials(0)
-        gate_tanh(0)
-        gate_sigmoid(0)
-        copy_values(1, 0)
-        scores(1)
-        gate_channels(0)
+        copy_values(0, 1)
+        quantise_queries(1)
+        quantise_keys(1, LEFT)
+        quantise_keys(1, RIGHT)
         turn_weights(0)
         gather_scales(1)
+        scores(1, LEFT)
+        scale_column(0)
+        scores(1, RIGHT)
         invert_sums(0)
-        scale_scores(1)
-        turn_scales(1)
-        maximum(1)
+        gate_tanh(0)
+        scale_scores(1, LEFT)
+        scale_scores(1, RIGHT)
         scale_weights(0)
-        quantise_values(0)
+        turn_values(1, 1)
+        copy_values(1, 0)
+        maximum(1)
+        turn_scales(1)
         quantise_weights(0)
+        gate_tanh(1)
+        gate_channels(0)
+        quantise_values(0)
         copy_values(1, 1)
         quantise_values(1)
         exponentials(1)
         invert_sums(1)
         scale_column(1)
-        gate_tanh(1)
         turn_weights(1)
         scale_weights(1)
-        products(0)
-        gate_sigmoid(1)
-        gate_channels(1)
-        finish(0)
+        products(0, ALL)
+        finish(0, ALL)
         quantise_weights(1)
-        products(1)
-        finish(1)
+        gate_channels(1)
+        products(1, LEFT)
+        products(1, RIGHT)
+        finish(1, LEFT)
+        finish(1, RIGHT)

from contextlib import ExitStack

import concourse.mybir as mybir
from concourse.masks import make_identity

FLOPS = 2 * 2 * 2 * 128 * 512 * 512

F32 = mybir.dt.float32
BF16 = mybir.dt.bfloat16
U32 = mybir.dt.uint32
I32 = mybir.dt.int32
U16 = mybir.dt.uint16
U8 = mybir.dt.uint8
FP8X4 = mybir.dt.float8_e4m3fn_x4
MULT = mybir.AluOpType.mult
ADD = mybir.AluOpType.add
MAX = mybir.AluOpType.max
COPY = mybir.ActivationFunctionType.Copy
EXP = mybir.ActivationFunctionType.Exp
TANH = mybir.ActivationFunctionType.Tanh
AXIS_X = mybir.AxisListType.X

P = 128
B = 2
N = 512
T = 2048
SEG = T // B
D = 512
NQ = 128
HALF = SEG // 2
LIST = N // 16
ALL, LEFT, RIGHT = slice(0, N), slice(0, N // 2), slice(N // 2, N)


def tile_attend_x_mla_gate_seg_kernel(tc, qT, cT, ts, ch, og, offs, out):
    nc = tc.nc
    with ExitStack() as ctx:
        lists = ctx.enter_context(tc.tile_pool(name="lists", bufs=1))
        keep = ctx.enter_context(tc.tile_pool(name="keep", bufs=1))
        psum = ctx.enter_context(tc.psum_pool(name="psum", bufs=1))

        offsets = lists.tile([P, B * LIST], U16, name="offsets")

        def each(shape, dtype, name):
            return [keep.tile(shape, dtype, name=f"{name}{b}", align_bytes=64) for b in range(B)]

        raw = {(b, w, h): keep.tile([P, 2, HALF], F32, name=f"raw{b}{w}{h}") for b in range(B) for w in range(2) for h in range(2)}
        scale_tab = keep.tile([P, T], F32, name="scale_tab")
        q_raw = each([P, 4, NQ], F32, "q_raw")
        ch_sb = keep.tile([P, D], F32, name="ch_sb")
        og_sb = each([P, D], F32, "og_sb")
        pairs = [keep.tile([P, T, 2], BF16, name=f"pairs{w}", align_bytes=64) for w in range(2)]
        kb = each([P, N, 4], BF16, "kb")
        k_codes, k_scales = each([P, N], U32, "k_codes"), each([P, N], U8, "k_scales")
        q_bf = each([P, NQ, 4], BF16, "q_bf")
        q_codes, q_scales = each([P, NQ], U32, "q_codes"), each([P, NQ], U8, "q_scales")
        tsg = each([P, N], F32, "tsg")
        ts_col = each([P, 4, 1], F32, "ts_col")
        a = each([P, 4, P], F32, "a")
        neg_m = each([P, 1], F32, "neg_m")
        p = each([P, 4, P], F32, "p")
        l_half = each([P, 2], F32, "l_half")
        l_sum = each([P, 1], F32, "l_sum")
        inv_l = each([P, 1], F32, "inv_l")
        vb = each([P, D, 4], BF16, "vb")
        v_codes, v_scales = each([P, D], U32, "v_codes"), each([P, D], U8, "v_scales")
        wb = each([P, NQ, 4], BF16, "wb")
        w_codes, w_scales = each([P, NQ], U32, "w_codes"), each([P, NQ], U8, "w_scales")
        th = each([P, D], F32, "th")
        gate = each([P, D], F32, "gate")
        o = each([P, D], F32, "o")
        bank = {}

        ident = keep.tile([P, P], F32, name="ident")
        make_identity(nc, ident[:])
        warm = keep.tile([P, 1], F32, name="warm")
        warmed = keep.tile([P, 1], F32, name="warmed")

        def preload_exp():
            nc.vector.memset(warm[:], 0.0)
            nc.scalar.activation(out=warmed[:], in_=warm[:], func=EXP)

        def load_pair(b, w, h):
            n0 = b * SEG + h * HALF
            nc.sync.dma_start(out=raw[b, w, h][:], in_=cT.rearrange("(p t) n -> p t n", t=4)[:, 2 * w : 2 * w + 2, n0 : n0 + HALF])

        def load_scales(b):
            nc.sync.dma_start(out=scale_tab[:, b * SEG : (b + 1) * SEG], in_=ts[:, b * SEG : (b + 1) * SEG])

        def load_queries(b):
            nc.sync.dma_start(out=q_raw[b][:], in_=qT[b].rearrange("(p t) q -> p t q", t=4))

        def load_channels():
            nc.sync.dma_start(out=ch_sb[:], in_=ch)

        def load_gate(b):
            nc.sync.dma_start(out=og_sb[b][:], in_=og[b])

        def cast(engine, b, w, h):
            n0 = b * SEG + h * HALF
            dst = pairs[w][:, n0 : n0 + HALF, :]
            src = raw[b, w, h][:].rearrange("p e n -> p n e")
            if engine is nc.scalar:
                nc.scalar.activation(out=dst, in_=src, func=COPY)
            else:
                nc.vector.tensor_copy(out=dst, in_=src)

        def gather_pair(b, w):
            window = pairs[w][:].rearrange("p n e -> p (n e)").bitcast(U32)
            if b == 0:
                window = window[:, 0:SEG]
            dst = kb[b][:].rearrange("p n t -> p (n t)").bitcast(U32).rearrange("p (j s w) -> p w s j", j=4, w=2)[:, w]
            nc.vector.tensor_copy(dst, window.indirect(offsets[:, b * LIST : (b + 1) * LIST]))

        def gather_scales(b):
            window = scale_tab[:].bitcast(U32)
            if b == 0:
                window = window[:, 0:SEG]
            nc.vector.tensor_copy(tsg[b][:].bitcast(U32).rearrange("p (j s) -> p s j", j=4), window.indirect(offsets[:, b * LIST : (b + 1) * LIST]))

        def turn_scales(b):
            bank["ts", b] = psum.tile([P, 4, P], F32, name="scale_bank", tag="scale_bank")
            for j in range(4):
                nc.tensor.transpose(bank["ts", b][:, j, :], tsg[b][:, j * P : (j + 1) * P], ident[:])

        def scale_column(b):
            nc.scalar.activation(out=ts_col[b][:], in_=bank["ts", b][:, :, 0:1], func=COPY)

        def cast_queries(b):
            nc.gpsimd.tensor_scalar(q_bf[b][:], q_raw[b][:].rearrange("p t q -> p q t"), 1.0, 0.0, MULT, ADD)

        def quantise(codes, scales, src):
            nc.vector.quantize_mx(out=codes[:].bitcast(FP8X4), scales=scales[:], in_=src[:].rearrange("p n t -> p (n t)"))

        def quantise_queries(b):
            quantise(q_codes[b], q_scales[b], q_bf[b])

        def quantise_keys(b, cols):
            nc.vector.quantize_mx(
                out=k_codes[b][:, cols].bitcast(FP8X4),
                scales=k_scales[b][:, cols],
                in_=kb[b][:, cols, :].rearrange("p n t -> p (n t)"),
            )

        def quantise_values(b):
            quantise(v_codes[b], v_scales[b], vb[b])

        def quantise_weights(b):
            quantise(w_codes[b], w_scales[b], wb[b])

        def scores(b, cols):
            tile = psum.tile([P, cols.stop - cols.start], F32, name="result", tag="result", bufs=3)
            bank["score", b, cols.start] = tile
            nc.tensor.matmul_mx(
                out=tile[:],
                lhsT=q_codes[b][:].bitcast(FP8X4),
                lhsT_scale=q_scales[b][:],
                rhs=k_codes[b][:, cols].bitcast(FP8X4),
                rhs_scale=k_scales[b][:, cols],
                start=True,
                stop=True,
            )

        def scale_scores(b, cols):
            flat = a[b][:].rearrange("q j s -> q (j s)")
            nc.vector.tensor_tensor(flat[:, cols], bank["score", b, cols.start][:], tsg[b][:, cols], MULT)

        def maximum(b):
            nc.vector.tensor_reduce(out=neg_m[b][:], in_=a[b][:].rearrange("q j s -> q (j s)"), axis=AXIS_X, op=MAX, negate=True)

        def exponentials(b):
            for h in range(2):
                j2 = slice(2 * h, 2 * h + 2)
                nc.scalar.activation(out=p[b][:, j2], in_=a[b][:, j2], func=EXP, bias=neg_m[b][:], accum_out=l_half[b][:, h : h + 1])

        def invert_sums(b):
            nc.gpsimd.tensor_scalar(l_sum[b][:], l_half[b][:, 0:1], l_half[b][:, 1:2], 2.0, ADD, MULT)
            nc.vector.reciprocal(inv_l[b][:], l_sum[b][:])

        def turn_values(b, w):
            bank["v", b, w] = psum.tile([P, 4, P], F32, name="value_bank", tag="value_bank", bufs=3)
            words = kb[b][:].rearrange("p n t -> p (n t)").bitcast(F32).rearrange("p (j s w) -> p w j s", j=4, w=2)
            for j in range(4):
                nc.tensor.transpose(bank["v", b, w][:, j, :], words[:, w, j, :], ident[:])

        def copy_values(b, w):
            src = bank["v", b, w][:].rearrange("s j p -> s (j p)").bitcast(BF16).rearrange("s (j p e) -> s p e j", j=4, e=2)
            nc.scalar.activation(out=vb[b][:].rearrange("s (p w e) j -> s w p e j", w=2, e=2)[:, w], in_=src, func=COPY)

        def turn_weights(b):
            bank["w", b] = psum.tile([P, 4, P], F32, name="weight_bank", tag="weight_bank")
            for j in range(4):
                nc.tensor.transpose(bank["w", b][:, j, :], p[b][:, j, :], ident[:])

        def scale_weights(b):
            nc.vector.tensor_tensor(
                wb[b][:],
                bank["w", b][:].rearrange("s j q -> s q j"),
                ts_col[b][:].rearrange("s j o -> s o j").to_broadcast([P, NQ, 4]),
                MULT,
            )

        def products(b, cols):
            tile = psum.tile([P, cols.stop - cols.start], F32, name="result", tag="result", bufs=3)
            bank["y", b, cols.start] = tile
            nc.tensor.matmul_mx(
                out=tile[:],
                lhsT=w_codes[b][:].bitcast(FP8X4),
                lhsT_scale=w_scales[b][:],
                rhs=v_codes[b][:, cols].bitcast(FP8X4),
                rhs_scale=v_scales[b][:, cols],
                start=True,
                stop=True,
            )

        def gate_tanh(b):
            nc.scalar.activation(out=th[b][:], in_=og_sb[b][:], func=TANH, scale=0.5)

        def gate_channels(b):
            nc.vector.scalar_tensor_tensor(out=gate[b][:], in0=th[b][:], scalar=1.0, in1=ch_sb[:], op0=ADD, op1=MULT)

        def finish(b, cols):
            y = bank["y", b, cols.start]
            nc.vector.scalar_tensor_tensor(out=o[b][:, cols], in0=y[:], scalar=inv_l[b][:], in1=gate[b][:, cols], op0=MULT, op1=MULT)
            nc.sync.dma_start(out=out[b][:, cols], in_=o[b][:, cols])

        load_pair(0, 0, 0)
        load_pair(0, 0, 1)
        nc.sync.dma_start(offsets[:], offs)
        load_pair(0, 1, 0)
        load_pair(0, 1, 1)
        load_queries(0)
        load_pair(1, 0, 0)
        load_pair(1, 0, 1)
        load_scales(0)
        load_pair(1, 1, 0)
        load_pair(1, 1, 1)
        load_queries(1)
        load_scales(1)
        load_channels()
        load_gate(0)
        load_gate(1)
        preload_exp()
        cast(nc.scalar, 0, 0, 0)
        cast(nc.vector, 0, 0, 1)
        cast(nc.scalar, 0, 1, 0)
        gather_pair(0, 0)
        cast_queries(0)
        cast(nc.vector, 0, 1, 1)
        turn_values(0, 0)
        gather_pair(0, 1)
        quantise_queries(0)
        quantise_keys(0, ALL)
        gather_scales(0)
        cast(nc.scalar, 1, 0, 0)
        scores(0, ALL)
        turn_values(0, 1)
        cast_queries(1)
        turn_scales(0)
        copy_values(0, 0)
        cast(nc.scalar, 1, 0, 1)
        scale_scores(0, ALL)
        cast(nc.scalar, 1, 1, 0)
        cast(nc.scalar, 1, 1, 1)
        gather_pair(1, 0)
        maximum(0)
        turn_values(1, 0)
        gather_pair(1, 1)
        exponentials(0)
        copy_values(0, 1)
        quantise_queries(1)
        quantise_keys(1, LEFT)
        quantise_keys(1, RIGHT)
        turn_weights(0)
        gather_scales(1)
        scores(1, LEFT)
        scale_column(0)
        scores(1, RIGHT)
        invert_sums(0)
        gate_tanh(0)
        scale_scores(1, LEFT)
        scale_scores(1, RIGHT)
        scale_weights(0)
        turn_values(1, 1)
        copy_values(1, 0)
        maximum(1)
        turn_scales(1)
        quantise_weights(0)
        gate_tanh(1)
        gate_channels(0)
        quantise_values(0)
        copy_values(1, 1)
        quantise_values(1)
        exponentials(1)
        invert_sums(1)
        scale_column(1)
        turn_weights(1)
        scale_weights(1)
        products(0, ALL)
        finish(0, ALL)
        quantise_weights(1)
        gate_channels(1)
        products(1, LEFT)
        products(1, RIGHT)
        finish(1, LEFT)
        finish(1, RIGHT)
